import numpy as np
import ml_dtypes


def mxq(x, axis, fmt="e4m3"):
    dtype, down = {"e4m3": (ml_dtypes.float8_e4m3fn, 7), "e5m2": (ml_dtypes.float8_e5m2, 14)}[fmt]
    v = np.moveaxis(np.asarray(x, np.float32).astype(ml_dtypes.bfloat16).astype(np.float64), axis, -1)
    blocks = v.reshape(v.shape[:-1] + (-1, 32))
    amax = np.abs(blocks).max(-1, keepdims=True)
    byte = np.maximum(np.where(amax > 0, np.frexp(amax)[1] - 1 + 127, 0) - down, 1)
    scale = np.exp2(byte - 127.0)
    codes = (blocks / scale).astype(np.float32).astype(dtype).astype(np.float64)
    return np.moveaxis((codes * scale).reshape(v.shape), -1, axis)


WIDE = False


def mx_kscale(k):
    if not WIDE:
        return np.ones(k)
    levels = np.array([10, -10, 5, -5, 0])
    if k % 512:
        return np.exp2(np.random.permutation(np.resize(levels, k // 32))).repeat(32)
    a = np.empty((k // 512, 16))
    for p in range(k // 512):
        a[p, :8] = np.random.permutation(np.resize(levels, 8))
        for g in range(8):
            far = levels[np.abs(levels - a[p, g]) >= 10]
            a[p, g + 8] = far[np.random.randint(len(far))]
    return np.exp2(a.ravel()).repeat(32)


def f64(x):
    return np.asarray(x).astype(np.float64)


def striped(idx):
    return np.tile(idx.reshape(-1, 16).T, (8, 1)).astype(np.uint16)


def unstriped(offs):
    return offs[:16].T.reshape(-1).astype(np.int64)


def striped8(idx):
    return np.concatenate([x.reshape(-1, 16).T for x in idx]).astype(np.uint16)


def runs(offs, k):
    lists = np.stack([offs[16 * r : 16 * r + 16].T.reshape(-1) for r in range(8)]).astype(np.int64)
    return lists[np.arange(k) % 512 // 64]


def pack_weight(w):
    k, n = w.shape
    w = f64(np.asarray(w, np.float32).astype(ml_dtypes.bfloat16)).reshape(k // 32, 32, n)
    amax = np.abs(w).max(1)
    byte = np.clip(np.where(amax > 0, np.frexp(amax)[1] - 1 + 127 - 7, 1), 1, 254)
    scaled = (w * np.exp2(127.0 - byte)[:, None, :]).reshape(k, n).astype(np.float32)
    words = np.ascontiguousarray(scaled.reshape(k // 512, 128, 4, n).transpose(0, 1, 3, 2)).astype(ml_dtypes.float8_e4m3fn).view(np.uint8)
    return words, np.ascontiguousarray(byte.astype(np.uint8).reshape(k // 512, 16, n))


def unpack_weight(words, scales):
    g, p, n, _ = words.shape
    vals = np.ascontiguousarray(words).view(ml_dtypes.float8_e4m3fn).astype(np.float64) * np.repeat(np.exp2(scales.astype(np.float64) - 127.0), 8, axis=1)[..., None]
    return vals.transpose(0, 1, 3, 2).reshape(g * 512, n)


def sigmoid(v):
    return 1.0 / (1.0 + np.exp(-np.maximum(v, -700.0)))


K, T, S, N, G, H, W, U = 512, 1024, 256, 512, 2048, 512, 128, 512


def setup_inputs():
    n = np.random.standard_normal
    s = mx_kscale(K)[:, None]
    u = mx_kscale(K)
    packed_xT = pack_weight(n((K, T)) * s)
    packed_dT = pack_weight(n((K, G)) / s)
    perm = np.random.permutation(S)
    perm2 = np.random.permutation(S)
    perm3 = np.random.permutation(U)
    return {
        "x_words": packed_xT[0],
        "x_scales": packed_xT[1],
        "d_words": packed_dT[0],
        "d_scales": packed_dT[1],
        "sl": np.random.uniform(1.0, 2.0, (H, 1)).astype(np.float32),
        "th": (0.5 * n((H, 1))).astype(np.float32),
        "gn": (np.random.uniform(0.5, 1.5, (H, 1)) * u[:, None]).astype(np.float32),
        "w1": (n((H, N)) / np.sqrt(2 * H) / u[:, None]).astype(np.float32),
        "w2": (n((K, N)) / np.sqrt(2 * K) / s).astype(np.float32),
        "offs": striped(np.random.permutation(T)[:S]),
        "ci": striped(np.random.permutation(G)[:H]),
        "n1": striped(np.random.permutation(S)),
        "n2": striped(perm[:W]),
        "n3": striped(perm[W:]),
        "n4": striped(perm2[:W]),
        "n5": striped(perm2[W:]),
        "hz": striped8(np.random.randint(0, T, (8, S))),
        "n6": striped(perm3[:S]),
        "n7": striped(perm3[S:]),
        "n8": striped(np.random.permutation(S)),
    }


def reference(x_words, x_scales, d_words, d_scales, sl, th, gn, w1, w2, offs, ci, n1, n2, n3, n4, n5, hz, n6, n7, n8):
    d_ci = unpack_weight(d_words, d_scales)[:, unstriped(ci)]
    xq = unpack_weight(x_words, x_scales)[:, unstriped(offs)]
    s = 0.0625 * (d_ci.T @ xq)
    sg = sigmoid(f64(sl) * (s[:, unstriped(n1)] - f64(th)))
    st = s * sg
    pa = st[:, unstriped(n2)]
    pb = st[:, unstriped(n3)]
    rb = pa - pb
    ra = np.maximum(pa, pb)
    ua = np.zeros((H, S))
    ua[:, unstriped(n4)] = ra
    ub = ua.copy()
    ub[:, unstriped(n5)] = rb
    z = f64(gn) * ub
    x_hz = unpack_weight(x_words, x_scales)[np.arange(K)[:, None], runs(hz, K)]
    h2 = mxq(f64(w1), 0, "e4m3").T @ mxq(z, 0, "e4m3") + mxq(f64(w2), 0, "e4m3").T @ x_hz
    dn = np.minimum(h2, h2[:, unstriped(n8)])
    up = np.maximum(h2, h2[:, unstriped(n8)])
    ph = np.zeros((N, U))
    ph[:, unstriped(n6)] = up
    out = ph.copy()
    out[:, unstriped(n7)] = dn
    return out

@@ -1,0 +1,263 @@
+from contextlib import ExitStack
+
+import concourse.mybir as mybir
+
+K, T, S, N, G, H, W, U = 512, 1024, 256, 512, 2048, 512, 128, 512
+FLOPS = 2 * K * H * S + 2 * H * N * S + 2 * K * N * S
+
+F32 = mybir.dt.float32
+BF16 = mybir.dt.bfloat16
+I32 = mybir.dt.int32
+U32 = mybir.dt.uint32
+U16 = mybir.dt.uint16
+U8 = mybir.dt.uint8
+FP8X4 = mybir.dt.float8_e4m3fn_x4
+ALU = mybir.AluOpType
+ACT = mybir.ActivationFunctionType
+
+P = 128
+PACK = 4
+HALF = S // 2
+SPARE = 16
+
+
+def tile_picked_xtznhecpxpagmx_none_p_kernel(
+    tc, x_words, x_scales, d_words, d_scales, sl, th, gn, w1, w2, offs, ci, n1, n2, n3, n4, n5, hz, n6, n7, n8, out
+):
+    nc = tc.nc
+    with ExitStack() as ctx:
+        lists = ctx.enter_context(tc.tile_pool(name="lists", bufs=1))
+        keep = ctx.enter_context(tc.tile_pool(name="keep", bufs=1))
+        psum = ctx.enter_context(tc.psum_pool(name="psum", bufs=1))
+
+        def sb(name, shape, dtype):
+            return keep.tile(shape, dtype, name=name, align_bytes=64)
+
+        def bank(number, name, width):
+            return psum.tile([P, width], F32, name=name, tag="bank%d" % number)
+
+        def load_list(name, src):
+            tile = lists.tile(list(src.shape), U16, name=name)
+            nc.sync.dma_start(tile[:], src)
+            return tile
+
+        def load_words(name, src, width):
+            tile = sb(name, [P, width], U32)
+            nc.sync.dma_start(tile[:].bitcast(I32), src[0].rearrange("p n t -> p (n t)").bitcast(I32))
+            return tile
+
+        def load_plane(name, src, width):
+            tile = sb(name, [P, width], U8)
+            nc.vector.memset(tile[:].bitcast(I32), 0)
+            for q in range(4):
+                nc.scalar.dma_start(tile[32 * q : 32 * q + 4, :].bitcast(I32), src[0, 4 * q : 4 * q + 4, :].bitcast(I32))
+            return tile
+
+        def load_column(name, src):
+            tile = sb(name, [P, PACK], F32)
+            nc.gpsimd.dma_start(tile[:], src.rearrange("(p t) o -> p (t o)", t=PACK))
+            return tile
+
+        ci_t = load_list("ci_t", ci)
+        offs_t = load_list("offs_t", offs)
+        d_plane = load_plane("d_plane", d_scales, G)
+        d_win = load_words("d_win", d_words, G)
+        x_win = load_words("x_win", x_words, T)
+        x_plane = load_plane("x_plane", x_scales, T)
+        sl_t = load_column("sl_t", sl)
+        th_t = load_column("th_t", th)
+        gn_t = load_column("gn_t", gn)
+        n1_t = load_list("n1_t", n1)
+        n2_t = load_list("n2_t", n2)
+        n3_t = load_list("n3_t", n3)
+        n4_t = load_list("n4_t", n4)
+        n5_t = load_list("n5_t", n5)
+        hz_t = load_list("hz_t", hz)
+        x_runs = sb("x_runs", [P, T], U8)
+        nc.vector.memset(x_runs[:].bitcast(I32), 0)
+        nc.sync.dma_start(x_runs[0:P:8, :].bitcast(I32), x_scales[0].bitcast(I32))
+        w_raw = []
+        for name, w in (("w2_raw", w2), ("w1_raw", w1)):
+            tile = sb(name, [P, PACK, N], F32)
+            nc.sync.dma_start(tile[:], w.rearrange("(p j) m -> p j m", j=PACK))
+            w_raw.append(tile)
+        n8_t = load_list("n8_t", n8)
+        n6_t = load_list("n6_t", n6)
+        n7_t = load_list("n7_t", n7)
+
+        d_sc = sb("d_sc", [P, H], U8)
+        nc.vector.tensor_copy(d_sc[:].rearrange("p (t s) -> p s t", t=PACK), d_plane[:].indirect(ci_t[:]))
+        x_sc = sb("x_sc", [P, S], U8)
+        nc.vector.tensor_copy(x_sc[:], x_plane[:].indirect(offs_t[:]))
+        d_q = sb("d_q", [P, H], U32)
+        nc.vector.tensor_copy(d_q[:].rearrange("p (t s) -> p s t", t=PACK), d_win[:].indirect(ci_t[:]))
+        x_q = sb("x_q", [P, S], U32)
+        for a in range(2):
+            nc.vector.tensor_copy(x_q[:, a * HALF : (a + 1) * HALF], x_win[:].indirect(offs_t[:, a * 8 : (a + 1) * 8]))
+        bias_t = sb("bias_t", [P, PACK], F32)
+        nc.vector.scalar_tensor_tensor(bias_t[:], sl_t[:], -1.0, th_t[:], ALU.mult, ALU.mult)
+
+        def mx(acc, lq, ls, lcols, rq, rs, rcols, start, stop):
+            nc.tensor.matmul_mx(
+                out=acc,
+                lhsT=lq[:, lcols].bitcast(FP8X4),
+                lhsT_scale=ls[:, lcols],
+                rhs=rq[:, rcols].bitcast(FP8X4),
+                rhs_scale=rs[:, rcols],
+                start=start,
+                stop=stop,
+            )
+
+        halves = [slice(0, HALF), slice(HALF, S)]
+        whole = slice(0, S)
+        s_t = [sb("s%d" % t, [P, S], F32) for t in range(PACK)]
+
+        def scores(t):
+            rows = slice(t * P, (t + 1) * P)
+            if t == 0:
+                for a in range(2):
+                    acc = bank(a, "s0_%d" % a, HALF)
+                    mx(acc[:], d_q, d_sc, rows, x_q, x_sc, halves[a], True, True)
+                    if a == 0:
+                        nc.scalar.activation(s_t[0][:, halves[0]], acc[:], ACT.Copy, scale=0.0625)
+                    else:
+                        nc.vector.tensor_scalar(s_t[0][:, halves[1]], acc[:], 0.0625, None, ALU.mult)
+            else:
+                acc = bank(1 + t, "s_acc%d" % t, S)
+                mx(acc[:], d_q, d_sc, rows, x_q, x_sc, whole, True, True)
+                nc.vector.tensor_scalar(s_t[t][:], acc[:], 0.0625, None, ALU.mult)
+
+        st_t = [sb("st%d" % t, [P, S], F32) for t in range(PACK)]
+        pair_t = [sb("pair%d" % t, [P, 2, W], F32) for t in range(PACK)]
+        z_half = [sb("z_half%d" % a, [P, HALF, PACK], BF16) for a in range(2)]
+
+        def gate(t):
+            sg = sb("sg%d" % t, [P, S], F32)
+            for a in range(2):
+                nc.scalar.activation(
+                    sg[:, halves[a]],
+                    s_t[t][:].indirect(n1_t[:, a * 8 : (a + 1) * 8]),
+                    ACT.Sigmoid,
+                    scale=sl_t[:, t : t + 1],
+                    bias=bias_t[:, t : t + 1],
+                )
+            nc.vector.tensor_tensor(st_t[t][:], s_t[t][:], sg[:], ALU.mult)
+
+        def pair(t):
+            pa = sb("pa%d" % t, [P, W], F32)
+            pb = sb("pb%d" % t, [P, W], F32)
+            nc.scalar.activation(pa[:], st_t[t][:].indirect(n2_t[:]), ACT.Copy)
+            nc.scalar.activation(pb[:], st_t[t][:].indirect(n3_t[:]), ACT.Copy)
+            nc.vector.tensor_tensor(pair_t[t][:, 0, :], pa[:], pb[:], ALU.max)
+            nc.vector.tensor_tensor(pair_t[t][:, 1, :], pa[:], pb[:], ALU.subtract)
+
+        def place(t):
+            ub = sb("ub%d" % t, [P, S], F32)
+            nc.scalar.activation(ub[:].indirect(n4_t[:]), pair_t[t][:, 0, :], ACT.Copy)
+            nc.scalar.activation(ub[:].indirect(n5_t[:]), pair_t[t][:, 1, :], ACT.Copy)
+            for a in range(2):
+                nc.vector.tensor_scalar(z_half[a][:, :, t], ub[:, halves[a]], gn_t[:, t : t + 1], None, ALU.mult)
+
+        w_q = {}
+
+        def weights(which, m):
+            grouped = sb("wg%d_%d" % (which, m), [P, P, PACK], BF16)
+            nc.vector.tensor_copy(
+                grouped[:].rearrange("p (c i) t -> p c t i", i=4),
+                w_raw[which][:, :, m * P : (m + 1) * P].rearrange("p t (c i) -> p c t i", i=4),
+            )
+            codes = sb("wq%d_%d" % (which, m), [P, P], U32)
+            plane = sb("ws%d_%d" % (which, m), [P, P], U8)
+            nc.vector.quantize_mx(out=codes[:].bitcast(FP8X4), scales=plane[:], in_=grouped[:].rearrange("p c t -> p (c t)"))
+            w_q[which, m] = (codes, plane)
+
+        hz_q = sb("hz_q", [P, S], U32)
+        hz_sc = sb("hz_sc", [P, S], U8)
+
+        def hashed():
+            picked = sb("hz_rows", [P, S], U8)
+            nc.vector.tensor_copy(picked[:], x_runs[:].indirect(hz_t[:]))
+            nc.vector.tensor_copy(hz_sc[:].bitcast(I32), picked[:].bitcast(I32))
+            for r in range(1, 4):
+                nc.sync.dma_start(hz_sc[r:P:32, :].bitcast(I32), picked[8 * r : P : 32, :].bitcast(I32))
+            nc.vector.tensor_copy(hz_q[:], x_win[:].indirect(hz_t[:]))
+
+        for t in range(PACK):
+            scores(t)
+        gate(0)
+        gate(1)
+        pair(0)
+        gate(2)
+        pair(1)
+        hashed()
+        place(0)
+        gate(3)
+        pair(2)
+        weights(0, 0)
+        place(1)
+        pair(3)
+        weights(1, 0)
+        weights(0, 1)
+        place(2)
+        weights(1, 1)
+        place(3)
+
+        z_q = sb("z_q", [P, S], U32)
+        z_sc = sb("z_sc", [P, S], U8)
+        for a in range(2):
+            nc.vector.quantize_mx(
+                out=z_q[:, halves[a]].bitcast(FP8X4), scales=z_sc[:, halves[a]], in_=z_half[a][:].rearrange("p c t -> p (c t)")
+            )
+
+        h_t = [sb("h%d" % m, [P, S + SPARE], F32) for m in range(4)]
+        for m in range(4):
+            nc.gpsimd.memset(h_t[m][:, S:], 0.0)
+        cols = slice(0, P)
+
+        def dense(m):
+            q2, s2 = w_q[0, m]
+            q1, s1 = w_q[1, m]
+            if m == 0:
+                accs = [bank(5 + a, "h0_%d" % a, HALF) for a in range(2)]
+                for a in range(2):
+                    mx(accs[a][:], q2, s2, cols, hz_q, hz_sc, halves[a], True, False)
+                for a in range(2):
+                    mx(accs[a][:], q1, s1, cols, z_q, z_sc, halves[a], False, True)
+                nc.scalar.activation(h_t[0][:, halves[0]], accs[0][:], ACT.Copy)
+                nc.vector.tensor_copy(h_t[0][:, halves[1]], accs[1][:])
+            else:
+                acc = bank((6 + m) % 8, "h_acc%d" % m, S)
+                mx(acc[:], q2, s2, cols, hz_q, hz_sc, whole, True, False)
+                mx(acc[:], q1, s1, cols, z_q, z_sc, whole, False, True)
+                nc.vector.tensor_copy(h_t[m][:, 0:S], acc[:])
+
+        ends = [sb("ends%d" % m, [P, 2, S], F32) for m in range(4)]
+
+        def compare(m):
+            other = sb("other%d" % m, [P, S], F32)
+            nc.scalar.activation(other[:], h_t[m][:].indirect(n8_t[:]), ACT.Copy)
+            nc.vector.tensor_tensor(ends[m][:, 0, :], h_t[m][:, 0:S], other[:], ALU.max)
+            nc.vector.tensor_tensor(ends[m][:, 1, :], h_t[m][:, 0:S], other[:], ALU.min)
+
+        def page(m):
+            pg = sb("page%d" % m, [P, U], F32)
+            nc.scalar.activation(pg[:].indirect(n6_t[:]), ends[m][:, 0, :], ACT.Copy)
+            nc.scalar.activation(pg[:].indirect(n7_t[:]), ends[m][:, 1, :], ACT.Copy)
+            nc.sync.dma_start(out[m * P : (m + 1) * P, :], pg[:])
+
+        dense(0)
+        dense(1)
+        compare(0)
+        compare(1)
+        weights(0, 2)
+        weights(1, 2)
+        dense(2)
+        page(0)
+        weights(0, 3)
+        weights(1, 3)
+        dense(3)
+        compare(2)
+        page(1)
+        compare(3)
+        page(2)
+        page(3)

@@ -19,6 +19,7 @@ P = 128
 PACK = 4
 HALF = S // 2
 SPARE = 16
+FIRST = 1024
 
 
 def tile_picked_xtznhecpxpagmx_none_p_kernel(
@@ -32,6 +33,9 @@ def tile_picked_xtznhecpxpagmx_none_p_kernel(
 
         def sb(name, shape, dtype):
             return keep.tile(shape, dtype, name=name, align_bytes=64)
+
+        def staged(slot, name, shape, dtype):
+            return keep.tile(shape, dtype, name=name, tag="stage%d" % slot, align_bytes=64)
 
         def bank(number, name, width):
             return psum.tile([P, width], F32, name=name, tag="bank%d" % number)
@@ -50,7 +54,7 @@ def tile_picked_xtznhecpxpagmx_none_p_kernel(
             tile = sb(name, [P, width], U8)
             nc.vector.memset(tile[:].bitcast(I32), 0)
             for q in range(4):
-                nc.scalar.dma_start(tile[32 * q : 32 * q + 4, :].bitcast(I32), src[0, 4 * q : 4 * q + 4, :].bitcast(I32))
+                nc.sync.dma_start(tile[32 * q : 32 * q + 4, :].bitcast(I32), src[0, 4 * q : 4 * q + 4, :].bitcast(I32))
             return tile
 
         def load_column(name, src):
@@ -58,44 +62,60 @@ def tile_picked_xtznhecpxpagmx_none_p_kernel(
             nc.gpsimd.dma_start(tile[:], src.rearrange("(p t) o -> p (t o)", t=PACK))
             return tile
 
+        warm_in = sb("warm_in", [P, 1], F32)
+        warm_out = sb("warm_out", [P, 1], F32)
+        nc.gpsimd.memset(warm_in[:], 0.0)
+        nc.scalar.activation(warm_out[:], warm_in[:], ACT.Sigmoid)
+
         ci_t = load_list("ci_t", ci)
-        offs_t = load_list("offs_t", offs)
+        d_win = sb("d_win", [P, G], U32)
+        d_src = d_words[0].rearrange("p n t -> p (n t)").bitcast(I32)
+        nc.sync.dma_start(d_win[:, :FIRST].bitcast(I32), d_src[:, :FIRST])
         d_plane = load_plane("d_plane", d_scales, G)
-        d_win = load_words("d_win", d_words, G)
-        x_win = load_words("x_win", x_words, T)
+        nc.sync.dma_start(d_win[:, FIRST:].bitcast(I32), d_src[:, FIRST:])
+        offs_t = load_list("offs_t", offs)
         x_plane = load_plane("x_plane", x_scales, T)
-        sl_t = load_column("sl_t", sl)
-        th_t = load_column("th_t", th)
-        gn_t = load_column("gn_t", gn)
         n1_t = load_list("n1_t", n1)
-        n2_t = load_list("n2_t", n2)
-        n3_t = load_list("n3_t", n3)
-        n4_t = load_list("n4_t", n4)
-        n5_t = load_list("n5_t", n5)
+        x_win = load_words("x_win", x_words, T)
+        th_t = load_column("th_t", th)
+        sl_t = load_column("sl_t", sl)
+        gn_t = load_column("gn_t", gn)
+        neg_th = sb("neg_th", [P, PACK], F32)
+        nc.gpsimd.tensor_scalar(neg_th[:], th_t[:], -1.0, 0.0, ALU.mult, ALU.add)
+        bias_t = sb("bias_t", [P, PACK], F32)
+        nc.gpsimd.tensor_tensor(bias_t[:], sl_t[:], neg_th[:], ALU.mult)
         hz_t = load_list("hz_t", hz)
         x_runs = sb("x_runs", [P, T], U8)
         nc.vector.memset(x_runs[:].bitcast(I32), 0)
         nc.sync.dma_start(x_runs[0:P:8, :].bitcast(I32), x_scales[0].bitcast(I32))
-        w_raw = []
-        for name, w in (("w2_raw", w2), ("w1_raw", w1)):
-            tile = sb(name, [P, PACK, N], F32)
-            nc.sync.dma_start(tile[:], w.rearrange("(p j) m -> p j m", j=PACK))
-            w_raw.append(tile)
+        n2_t = load_list("n2_t", n2)
+        n3_t = load_list("n3_t", n3)
+        w_raw = {}
+
+        def load_weights(part):
+            for which, w in enumerate((w2, w1)):
+                tile = sb("w_raw%d_%d" % (which, part), [P, PACK, N // 2], F32)
+                src = w.rearrange("(p j) m -> p j m", j=PACK)
+                nc.sync.dma_start(tile[:], src[:, :, part * (N // 2) : (part + 1) * (N // 2)])
+                w_raw[which, part] = tile
+
+        load_weights(0)
+        n4_t = load_list("n4_t", n4)
+        n5_t = load_list("n5_t", n5)
         n8_t = load_list("n8_t", n8)
         n6_t = load_list("n6_t", n6)
         n7_t = load_list("n7_t", n7)
+        load_weights(1)
 
-        d_sc = sb("d_sc", [P, H], U8)
+        d_sc = staged(2, "d_sc", [P, H], U8)
         nc.vector.tensor_copy(d_sc[:].rearrange("p (t s) -> p s t", t=PACK), d_plane[:].indirect(ci_t[:]))
+        d_q = staged(3, "d_q", [P, H], U32)
+        nc.vector.tensor_copy(d_q[:].rearrange("p (t s) -> p s t", t=PACK), d_win[:].indirect(ci_t[:]))
         x_sc = sb("x_sc", [P, S], U8)
         nc.vector.tensor_copy(x_sc[:], x_plane[:].indirect(offs_t[:]))
-        d_q = sb("d_q", [P, H], U32)
-        nc.vector.tensor_copy(d_q[:].rearrange("p (t s) -> p s t", t=PACK), d_win[:].indirect(ci_t[:]))
         x_q = sb("x_q", [P, S], U32)
         for a in range(2):
             nc.vector.tensor_copy(x_q[:, a * HALF : (a + 1) * HALF], x_win[:].indirect(offs_t[:, a * 8 : (a + 1) * 8]))
-        bias_t = sb("bias_t", [P, PACK], F32)
-        nc.vector.scalar_tensor_tensor(bias_t[:], sl_t[:], -1.0, th_t[:], ALU.mult, ALU.mult)
 
         def mx(acc, lq, ls, lcols, rq, rs, rcols, start, stop):
             nc.tensor.matmul_mx(
@@ -110,7 +130,9 @@ def tile_picked_xtznhecpxpagmx_none_p_kernel(
 
         halves = [slice(0, HALF), slice(HALF, S)]
         whole = slice(0, S)
-        s_t = [sb("s%d" % t, [P, S], F32) for t in range(PACK)]
+        s_t = [sb("s%d" % t, [P, 2 * S], F32) for t in range(PACK)]
+        for t in range(PACK):
+            nc.vector.memset(s_t[t][:, S:], 0.0)
 
         def scores(t):
             rows = slice(t * P, (t + 1) * P)
@@ -118,64 +140,61 @@ def tile_picked_xtznhecpxpagmx_none_p_kernel(
                 for a in range(2):
                     acc = bank(a, "s0_%d" % a, HALF)
                     mx(acc[:], d_q, d_sc, rows, x_q, x_sc, halves[a], True, True)
-                    if a == 0:
-                        nc.scalar.activation(s_t[0][:, halves[0]], acc[:], ACT.Copy, scale=0.0625)
-                    else:
-                        nc.vector.tensor_scalar(s_t[0][:, halves[1]], acc[:], 0.0625, None, ALU.mult)
+                    nc.scalar.activation(s_t[0][:, halves[a]], acc[:], ACT.Copy, scale=0.0625)
             else:
                 acc = bank(1 + t, "s_acc%d" % t, S)
                 mx(acc[:], d_q, d_sc, rows, x_q, x_sc, whole, True, True)
-                nc.vector.tensor_scalar(s_t[t][:], acc[:], 0.0625, None, ALU.mult)
+                nc.vector.tensor_scalar(s_t[t][:, whole], acc[:], 0.0625, None, ALU.mult)
 
         st_t = [sb("st%d" % t, [P, S], F32) for t in range(PACK)]
         pair_t = [sb("pair%d" % t, [P, 2, W], F32) for t in range(PACK)]
-        z_half = [sb("z_half%d" % a, [P, HALF, PACK], BF16) for a in range(2)]
+        z_half = []
 
         def gate(t):
             sg = sb("sg%d" % t, [P, S], F32)
-            for a in range(2):
-                nc.scalar.activation(
-                    sg[:, halves[a]],
-                    s_t[t][:].indirect(n1_t[:, a * 8 : (a + 1) * 8]),
-                    ACT.Sigmoid,
-                    scale=sl_t[:, t : t + 1],
-                    bias=bias_t[:, t : t + 1],
-                )
-            nc.vector.tensor_tensor(st_t[t][:], s_t[t][:], sg[:], ALU.mult)
+            nc.scalar.activation(
+                sg[:], s_t[t][:].indirect(n1_t[:]), ACT.Sigmoid, scale=sl_t[:, t : t + 1], bias=bias_t[:, t : t + 1]
+            )
+            nc.vector.tensor_tensor(st_t[t][:], s_t[t][:, whole], sg[:], ALU.mult)
 
         def pair(t):
-            pa = sb("pa%d" % t, [P, W], F32)
+            pa = staged(t - 1, "pa%d" % t, [P, W], F32) if t in (1, 2) else sb("pa%d" % t, [P, W], F32)
             pb = sb("pb%d" % t, [P, W], F32)
             nc.scalar.activation(pa[:], st_t[t][:].indirect(n2_t[:]), ACT.Copy)
             nc.scalar.activation(pb[:], st_t[t][:].indirect(n3_t[:]), ACT.Copy)
             nc.vector.tensor_tensor(pair_t[t][:, 0, :], pa[:], pb[:], ALU.max)
             nc.vector.tensor_tensor(pair_t[t][:, 1, :], pa[:], pb[:], ALU.subtract)
 
-        def place(t):
-            ub = sb("ub%d" % t, [P, S], F32)
-            nc.scalar.activation(ub[:].indirect(n4_t[:]), pair_t[t][:, 0, :], ACT.Copy)
-            nc.scalar.activation(ub[:].indirect(n5_t[:]), pair_t[t][:, 1, :], ACT.Copy)
+        ub_t = [sb("ub%d" % t, [P, S], F32) for t in range(PACK)]
+
+        def place(t, side):
+            nc.scalar.activation(ub_t[t][:].indirect((n4_t, n5_t)[side][:]), pair_t[t][:, side, :], ACT.Copy)
+
+        def gain(t):
             for a in range(2):
-                nc.vector.tensor_scalar(z_half[a][:, :, t], ub[:, halves[a]], gn_t[:, t : t + 1], None, ALU.mult)
+                nc.vector.tensor_scalar(z_half[a][:, :, t], ub_t[t][:, halves[a]], gn_t[:, t : t + 1], None, ALU.mult)
 
         w_q = {}
 
-        def weights(which, m):
-            grouped = sb("wg%d_%d" % (which, m), [P, P, PACK], BF16)
-            nc.vector.tensor_copy(
-                grouped[:].rearrange("p (c i) t -> p c t i", i=4),
-                w_raw[which][:, :, m * P : (m + 1) * P].rearrange("p t (c i) -> p c t i", i=4),
-            )
-            codes = sb("wq%d_%d" % (which, m), [P, P], U32)
-            plane = sb("ws%d_%d" % (which, m), [P, P], U8)
-            nc.vector.quantize_mx(out=codes[:].bitcast(FP8X4), scales=plane[:], in_=grouped[:].rearrange("p c t -> p (c t)"))
-            w_q[which, m] = (codes, plane)
+        def weights(m, slot):
+            grouped = staged(slot, "wg%d" % m, [P, 2, P, PACK], BF16)
+            for which in range(2):
+                nc.vector.tensor_copy(
+                    grouped[:, which].rearrange("p (c i) t -> p c t i", i=4),
+                    w_raw[which, m // 2][:, :, (m % 2) * P : (m % 2 + 1) * P].rearrange("p t (c i) -> p c t i", i=4),
+                )
+            codes = sb("wq%d" % m, [P, 2 * P], U32)
+            plane = sb("ws%d" % m, [P, 2 * P], U8)
+            nc.vector.quantize_mx(out=codes[:].bitcast(FP8X4), scales=plane[:], in_=grouped[:].rearrange("p w c t -> p (w c t)"))
+            w_q[m] = (codes, plane)
 
-        hz_q = sb("hz_q", [P, S], U32)
+        hz_words = []
         hz_sc = sb("hz_sc", [P, S], U8)
 
         def hashed():
-            picked = sb("hz_rows", [P, S], U8)
+            picked = staged(2, "hz_rows", [P, S], U8)
+            hz_q = staged(3, "hz_q", [P, S], U32)
+            hz_words.append(hz_q)
             nc.vector.tensor_copy(picked[:], x_runs[:].indirect(hz_t[:]))
             nc.vector.tensor_copy(hz_sc[:].bitcast(I32), picked[:].bitcast(I32))
             for r in range(1, 4):
@@ -184,23 +203,20 @@ def tile_picked_xtznhecpxpagmx_none_p_kernel(
 
         for t in range(PACK):
             scores(t)
-        gate(0)
-        gate(1)
-        pair(0)
-        gate(2)
-        pair(1)
+        for t in range(PACK):
+            gate(t)
+        for t in range(PACK):
+            pair(t)
         hashed()
-        place(0)
-        gate(3)
-        pair(2)
-        weights(0, 0)
-        place(1)
-        pair(3)
-        weights(1, 0)
-        weights(0, 1)
-        place(2)
-        weights(1, 1)
-        place(3)
+        for m in range(4):
+            weights(m, m % 2)
+        for first in (0, 2):
+            for side in range(2):
+                for t in (first, first + 1):
+                    place(t, side)
+        z_half.extend(staged(a, "z_half%d" % a, [P, HALF, PACK], BF16) for a in range(2))
+        for t in range(PACK):
+            gain(t)
 
         z_q = sb("z_q", [P, S], U32)
         z_sc = sb("z_sc", [P, S], U8)
@@ -212,23 +228,23 @@ def tile_picked_xtznhecpxpagmx_none_p_kernel(
         h_t = [sb("h%d" % m, [P, S + SPARE], F32) for m in range(4)]
         for m in range(4):
             nc.gpsimd.memset(h_t[m][:, S:], 0.0)
-        cols = slice(0, P)
+        w2_cols, w1_cols = slice(0, P), slice(P, 2 * P)
 
         def dense(m):
-            q2, s2 = w_q[0, m]
-            q1, s1 = w_q[1, m]
+            wq, ws = w_q[m]
+            hz_q = hz_words[0]
             if m == 0:
                 accs = [bank(5 + a, "h0_%d" % a, HALF) for a in range(2)]
                 for a in range(2):
-                    mx(accs[a][:], q2, s2, cols, hz_q, hz_sc, halves[a], True, False)
+                    mx(accs[a][:], wq, ws, w2_cols, hz_q, hz_sc, halves[a], True, False)
                 for a in range(2):
-                    mx(accs[a][:], q1, s1, cols, z_q, z_sc, halves[a], False, True)
-                nc.scalar.activation(h_t[0][:, halves[0]], accs[0][:], ACT.Copy)
-                nc.vector.tensor_copy(h_t[0][:, halves[1]], accs[1][:])
+                    mx(accs[a][:], wq, ws, w1_cols, z_q, z_sc, halves[a], False, True)
+                for a in range(2):
+                    nc.scalar.activation(h_t[0][:, halves[a]], accs[a][:], ACT.Copy)
             else:
                 acc = bank((6 + m) % 8, "h_acc%d" % m, S)
-                mx(acc[:], q2, s2, cols, hz_q, hz_sc, whole, True, False)
-                mx(acc[:], q1, s1, cols, z_q, z_sc, whole, False, True)
+                mx(acc[:], wq, ws, w2_cols, hz_q, hz_sc, whole, True, False)
+                mx(acc[:], wq, ws, w1_cols, z_q, z_sc, whole, False, True)
                 nc.vector.tensor_copy(h_t[m][:, 0:S], acc[:])
 
         ends = [sb("ends%d" % m, [P, 2, S], F32) for m in range(4)]
@@ -236,28 +252,22 @@ def tile_picked_xtznhecpxpagmx_none_p_kernel(
         def compare(m):
             other = sb("other%d" % m, [P, S], F32)
             nc.scalar.activation(other[:], h_t[m][:].indirect(n8_t[:]), ACT.Copy)
-            nc.vector.tensor_tensor(ends[m][:, 0, :], h_t[m][:, 0:S], other[:], ALU.max)
-            nc.vector.tensor_tensor(ends[m][:, 1, :], h_t[m][:, 0:S], other[:], ALU.min)
+            here = h_t[m][:, 0:S]
+            nc.vector.tensor_tensor(ends[m][:, 0, :], here, other[:], ALU.max)
+            nc.vector.tensor_tensor(ends[m][:, 1, :], here, other[:], ALU.min)
 
-        def page(m):
-            pg = sb("page%d" % m, [P, U], F32)
-            nc.scalar.activation(pg[:].indirect(n6_t[:]), ends[m][:, 0, :], ACT.Copy)
-            nc.scalar.activation(pg[:].indirect(n7_t[:]), ends[m][:, 1, :], ACT.Copy)
-            nc.sync.dma_start(out[m * P : (m + 1) * P, :], pg[:])
+        pages = [sb("page%d" % m, [P, U], F32) for m in range(4)]
 
-        dense(0)
-        dense(1)
-        compare(0)
-        compare(1)
-        weights(0, 2)
-        weights(1, 2)
-        dense(2)
-        page(0)
-        weights(0, 3)
-        weights(1, 3)
-        dense(3)
-        compare(2)
-        page(1)
-        compare(3)
-        page(2)
-        page(3)
+        def page(m, side):
+            nc.scalar.activation(pages[m][:].indirect((n6_t, n7_t)[side][:]), ends[m][:, side, :], ACT.Copy)
+            if side == 1:
+                nc.sync.dma_start(out[m * P : (m + 1) * P, :], pages[m][:])
+
+        for m in range(4):
+            dense(m)
+        for m in range(4):
+            compare(m)
+        for first in (0, 2):
+            for side in range(2):
+                for m in (first, first + 1):
+                    page(m, side)

@@ -59,7 +59,7 @@ def tile_picked_xtznhecpxpagmx_none_p_kernel(
 
         def load_column(name, src):
             tile = sb(name, [P, PACK], F32)
-            nc.gpsimd.dma_start(tile[:], src.rearrange("(p t) o -> p (t o)", t=PACK))
+            nc.sync.dma_start(tile[:], src.rearrange("(p t) o -> p (t o)", t=PACK))
             return tile
 
         warm_in = sb("warm_in", [P, 1], F32)
@@ -79,7 +79,6 @@ def tile_picked_xtznhecpxpagmx_none_p_kernel(
         x_win = load_words("x_win", x_words, T)
         th_t = load_column("th_t", th)
         sl_t = load_column("sl_t", sl)
-        gn_t = load_column("gn_t", gn)
         neg_th = sb("neg_th", [P, PACK], F32)
         nc.gpsimd.tensor_scalar(neg_th[:], th_t[:], -1.0, 0.0, ALU.mult, ALU.add)
         bias_t = sb("bias_t", [P, PACK], F32)
@@ -102,6 +101,7 @@ def tile_picked_xtznhecpxpagmx_none_p_kernel(
         load_weights(0)
         n4_t = load_list("n4_t", n4)
         n5_t = load_list("n5_t", n5)
+        gn_t = load_column("gn_t", gn)
         n8_t = load_list("n8_t", n8)
         n6_t = load_list("n6_t", n6)
         n7_t = load_list("n7_t", n7)

from contextlib import ExitStack

import concourse.mybir as mybir

K, T, S, N, G, H, W, U = 512, 1024, 256, 512, 2048, 512, 128, 512
FLOPS = 2 * K * H * S + 2 * H * N * S + 2 * K * N * S

F32 = mybir.dt.float32
BF16 = mybir.dt.bfloat16
I32 = mybir.dt.int32
U32 = mybir.dt.uint32
U16 = mybir.dt.uint16
U8 = mybir.dt.uint8
FP8X4 = mybir.dt.float8_e4m3fn_x4
ALU = mybir.AluOpType
ACT = mybir.ActivationFunctionType

P = 128
PACK = 4
HALF = S // 2
SPARE = 16
FIRST = 1024


def tile_picked_xtznhecpxpagmx_none_p_kernel(
    tc, x_words, x_scales, d_words, d_scales, sl, th, gn, w1, w2, offs, ci, n1, n2, n3, n4, n5, hz, n6, n7, n8, out
):
    nc = tc.nc
    with ExitStack() as ctx:
        lists = ctx.enter_context(tc.tile_pool(name="lists", bufs=1))
        keep = ctx.enter_context(tc.tile_pool(name="keep", bufs=1))
        psum = ctx.enter_context(tc.psum_pool(name="psum", bufs=1))

        def sb(name, shape, dtype):
            return keep.tile(shape, dtype, name=name, align_bytes=64)

        def staged(slot, name, shape, dtype):
            return keep.tile(shape, dtype, name=name, tag="stage%d" % slot, align_bytes=64)

        def bank(number, name, width):
            return psum.tile([P, width], F32, name=name, tag="bank%d" % number)

        def load_list(name, src):
            tile = lists.tile(list(src.shape), U16, name=name)
            nc.sync.dma_start(tile[:], src)
            return tile

        def load_words(name, src, width):
            tile = sb(name, [P, width], U32)
            nc.sync.dma_start(tile[:].bitcast(I32), src[0].rearrange("p n t -> p (n t)").bitcast(I32))
            return tile

        def load_plane(name, src, width):
            tile = sb(name, [P, width], U8)
            nc.vector.memset(tile[:].bitcast(I32), 0)
            for q in range(4):
                nc.sync.dma_start(tile[32 * q : 32 * q + 4, :].bitcast(I32), src[0, 4 * q : 4 * q + 4, :].bitcast(I32))
            return tile

        def load_column(name, src):
            tile = sb(name, [P, PACK], F32)
            nc.sync.dma_start(tile[:], src.rearrange("(p t) o -> p (t o)", t=PACK))
            return tile

        warm_in = sb("warm_in", [P, 1], F32)
        warm_out = sb("warm_out", [P, 1], F32)
        nc.gpsimd.memset(warm_in[:], 0.0)
        nc.scalar.activation(warm_out[:], warm_in[:], ACT.Sigmoid)

        ci_t = load_list("ci_t", ci)
        d_win = sb("d_win", [P, G], U32)
        d_src = d_words[0].rearrange("p n t -> p (n t)").bitcast(I32)
        nc.sync.dma_start(d_win[:, :FIRST].bitcast(I32), d_src[:, :FIRST])
        d_plane = load_plane("d_plane", d_scales, G)
        nc.sync.dma_start(d_win[:, FIRST:].bitcast(I32), d_src[:, FIRST:])
        offs_t = load_list("offs_t", offs)
        x_plane = load_plane("x_plane", x_scales, T)
        n1_t = load_list("n1_t", n1)
        x_win = load_words("x_win", x_words, T)
        th_t = load_column("th_t", th)
        sl_t = load_column("sl_t", sl)
        neg_th = sb("neg_th", [P, PACK], F32)
        nc.gpsimd.tensor_scalar(neg_th[:], th_t[:], -1.0, 0.0, ALU.mult, ALU.add)
        bias_t = sb("bias_t", [P, PACK], F32)
        nc.gpsimd.tensor_tensor(bias_t[:], sl_t[:], neg_th[:], ALU.mult)
        hz_t = load_list("hz_t", hz)
        x_runs = sb("x_runs", [P, T], U8)
        nc.vector.memset(x_runs[:].bitcast(I32), 0)
        nc.sync.dma_start(x_runs[0:P:8, :].bitcast(I32), x_scales[0].bitcast(I32))
        n2_t = load_list("n2_t", n2)
        n3_t = load_list("n3_t", n3)
        w_raw = {}

        def load_weights(part):
            for which, w in enumerate((w2, w1)):
                tile = sb("w_raw%d_%d" % (which, part), [P, PACK, N // 2], F32)
                src = w.rearrange("(p j) m -> p j m", j=PACK)
                nc.sync.dma_start(tile[:], src[:, :, part * (N // 2) : (part + 1) * (N // 2)])
                w_raw[which, part] = tile

        load_weights(0)
        n4_t = load_list("n4_t", n4)
        n5_t = load_list("n5_t", n5)
        gn_t = load_column("gn_t", gn)
        n8_t = load_list("n8_t", n8)
        n6_t = load_list("n6_t", n6)
        n7_t = load_list("n7_t", n7)
        load_weights(1)

        d_sc = staged(2, "d_sc", [P, H], U8)
        nc.vector.tensor_copy(d_sc[:].rearrange("p (t s) -> p s t", t=PACK), d_plane[:].indirect(ci_t[:]))
        d_q = staged(3, "d_q", [P, H], U32)
        nc.vector.tensor_copy(d_q[:].rearrange("p (t s) -> p s t", t=PACK), d_win[:].indirect(ci_t[:]))
        x_sc = sb("x_sc", [P, S], U8)
        nc.vector.tensor_copy(x_sc[:], x_plane[:].indirect(offs_t[:]))
        x_q = sb("x_q", [P, S], U32)
        for a in range(2):
            nc.vector.tensor_copy(x_q[:, a * HALF : (a + 1) * HALF], x_win[:].indirect(offs_t[:, a * 8 : (a + 1) * 8]))

        def mx(acc, lq, ls, lcols, rq, rs, rcols, start, stop):
            nc.tensor.matmul_mx(
                out=acc,
                lhsT=lq[:, lcols].bitcast(FP8X4),
                lhsT_scale=ls[:, lcols],
                rhs=rq[:, rcols].bitcast(FP8X4),
                rhs_scale=rs[:, rcols],
                start=start,
                stop=stop,
            )

        halves = [slice(0, HALF), slice(HALF, S)]
        whole = slice(0, S)
        s_t = [sb("s%d" % t, [P, 2 * S], F32) for t in range(PACK)]
        for t in range(PACK):
            nc.vector.memset(s_t[t][:, S:], 0.0)

        def scores(t):
            rows = slice(t * P, (t + 1) * P)
            if t == 0:
                for a in range(2):
                    acc = bank(a, "s0_%d" % a, HALF)
                    mx(acc[:], d_q, d_sc, rows, x_q, x_sc, halves[a], True, True)
                    nc.scalar.activation(s_t[0][:, halves[a]], acc[:], ACT.Copy, scale=0.0625)
            else:
                acc = bank(1 + t, "s_acc%d" % t, S)
                mx(acc[:], d_q, d_sc, rows, x_q, x_sc, whole, True, True)
                nc.vector.tensor_scalar(s_t[t][:, whole], acc[:], 0.0625, None, ALU.mult)

        st_t = [sb("st%d" % t, [P, S], F32) for t in range(PACK)]
        pair_t = [sb("pair%d" % t, [P, 2, W], F32) for t in range(PACK)]
        z_half = []

        def gate(t):
            sg = sb("sg%d" % t, [P, S], F32)
            nc.scalar.activation(
                sg[:], s_t[t][:].indirect(n1_t[:]), ACT.Sigmoid, scale=sl_t[:, t : t + 1], bias=bias_t[:, t : t + 1]
            )
            nc.vector.tensor_tensor(st_t[t][:], s_t[t][:, whole], sg[:], ALU.mult)

        def pair(t):
            pa = staged(t - 1, "pa%d" % t, [P, W], F32) if t in (1, 2) else sb("pa%d" % t, [P, W], F32)
            pb = sb("pb%d" % t, [P, W], F32)
            nc.scalar.activation(pa[:], st_t[t][:].indirect(n2_t[:]), ACT.Copy)
            nc.scalar.activation(pb[:], st_t[t][:].indirect(n3_t[:]), ACT.Copy)
            nc.vector.tensor_tensor(pair_t[t][:, 0, :], pa[:], pb[:], ALU.max)
            nc.vector.tensor_tensor(pair_t[t][:, 1, :], pa[:], pb[:], ALU.subtract)

        ub_t = [sb("ub%d" % t, [P, S], F32) for t in range(PACK)]

        def place(t, side):
            nc.scalar.activation(ub_t[t][:].indirect((n4_t, n5_t)[side][:]), pair_t[t][:, side, :], ACT.Copy)

        def gain(t):
            for a in range(2):
                nc.vector.tensor_scalar(z_half[a][:, :, t], ub_t[t][:, halves[a]], gn_t[:, t : t + 1], None, ALU.mult)

        w_q = {}

        def weights(m, slot):
            grouped = staged(slot, "wg%d" % m, [P, 2, P, PACK], BF16)
            for which in range(2):
                nc.vector.tensor_copy(
                    grouped[:, which].rearrange("p (c i) t -> p c t i", i=4),
                    w_raw[which, m // 2][:, :, (m % 2) * P : (m % 2 + 1) * P].rearrange("p t (c i) -> p c t i", i=4),
                )
            codes = sb("wq%d" % m, [P, 2 * P], U32)
            plane = sb("ws%d" % m, [P, 2 * P], U8)
            nc.vector.quantize_mx(out=codes[:].bitcast(FP8X4), scales=plane[:], in_=grouped[:].rearrange("p w c t -> p (w c t)"))
            w_q[m] = (codes, plane)

        hz_words = []
        hz_sc = sb("hz_sc", [P, S], U8)

        def hashed():
            picked = staged(2, "hz_rows", [P, S], U8)
            hz_q = staged(3, "hz_q", [P, S], U32)
            hz_words.append(hz_q)
            nc.vector.tensor_copy(picked[:], x_runs[:].indirect(hz_t[:]))
            nc.vector.tensor_copy(hz_sc[:].bitcast(I32), picked[:].bitcast(I32))
            for r in range(1, 4):
                nc.sync.dma_start(hz_sc[r:P:32, :].bitcast(I32), picked[8 * r : P : 32, :].bitcast(I32))
            nc.vector.tensor_copy(hz_q[:], x_win[:].indirect(hz_t[:]))

        for t in range(PACK):
            scores(t)
        for t in range(PACK):
            gate(t)
        for t in range(PACK):
            pair(t)
        hashed()
        for m in range(4):
            weights(m, m % 2)
        for first in (0, 2):
            for side in range(2):
                for t in (first, first + 1):
                    place(t, side)
        z_half.extend(staged(a, "z_half%d" % a, [P, HALF, PACK], BF16) for a in range(2))
        for t in range(PACK):
            gain(t)

        z_q = sb("z_q", [P, S], U32)
        z_sc = sb("z_sc", [P, S], U8)
        for a in range(2):
            nc.vector.quantize_mx(
                out=z_q[:, halves[a]].bitcast(FP8X4), scales=z_sc[:, halves[a]], in_=z_half[a][:].rearrange("p c t -> p (c t)")
            )

        h_t = [sb("h%d" % m, [P, S + SPARE], F32) for m in range(4)]
        for m in range(4):
            nc.gpsimd.memset(h_t[m][:, S:], 0.0)
        w2_cols, w1_cols = slice(0, P), slice(P, 2 * P)

        def dense(m):
            wq, ws = w_q[m]
            hz_q = hz_words[0]
            if m == 0:
                accs = [bank(5 + a, "h0_%d" % a, HALF) for a in range(2)]
                for a in range(2):
                    mx(accs[a][:], wq, ws, w2_cols, hz_q, hz_sc, halves[a], True, False)
                for a in range(2):
                    mx(accs[a][:], wq, ws, w1_cols, z_q, z_sc, halves[a], False, True)
                for a in range(2):
                    nc.scalar.activation(h_t[0][:, halves[a]], accs[a][:], ACT.Copy)
            else:
                acc = bank((6 + m) % 8, "h_acc%d" % m, S)
                mx(acc[:], wq, ws, w2_cols, hz_q, hz_sc, whole, True, False)
                mx(acc[:], wq, ws, w1_cols, z_q, z_sc, whole, False, True)
                nc.vector.tensor_copy(h_t[m][:, 0:S], acc[:])

        ends = [sb("ends%d" % m, [P, 2, S], F32) for m in range(4)]

        def compare(m):
            other = sb("other%d" % m, [P, S], F32)
            nc.scalar.activation(other[:], h_t[m][:].indirect(n8_t[:]), ACT.Copy)
            here = h_t[m][:, 0:S]
            nc.vector.tensor_tensor(ends[m][:, 0, :], here, other[:], ALU.max)
            nc.vector.tensor_tensor(ends[m][:, 1, :], here, other[:], ALU.min)

        pages = [sb("page%d" % m, [P, U], F32) for m in range(4)]

        def page(m, side):
            nc.scalar.activation(pages[m][:].indirect((n6_t, n7_t)[side][:]), ends[m][:, side, :], ACT.Copy)
            if side == 1:
                nc.sync.dma_start(out[m * P : (m + 1) * P, :], pages[m][:])

        for m in range(4):
            dense(m)
        for m in range(4):
            compare(m)
        for first in (0, 2):
            for side in range(2):
                for m in (first, first + 1):
                    page(m, side)
